import numpy as np
import ml_dtypes


def mxq(x, axis, fmt="e4m3"):
    dtype, down = {"e4m3": (ml_dtypes.float8_e4m3fn, 7), "e5m2": (ml_dtypes.float8_e5m2, 14)}[fmt]
    v = np.moveaxis(np.asarray(x, np.float32).astype(ml_dtypes.bfloat16).astype(np.float64), axis, -1)
    blocks = v.reshape(v.shape[:-1] + (-1, 32))
    amax = np.abs(blocks).max(-1, keepdims=True)
    byte = np.maximum(np.where(amax > 0, np.frexp(amax)[1] - 1 + 127, 0) - down, 1)
    scale = np.exp2(byte - 127.0)
    codes = (blocks / scale).astype(np.float32).astype(dtype).astype(np.float64)
    return np.moveaxis((codes * scale).reshape(v.shape), -1, axis)


WIDE = False


def mx_kscale(k):
    if not WIDE:
        return np.ones(k)
    levels = np.array([10, -10, 5, -5, 0])
    if k % 512:
        return np.exp2(np.random.permutation(np.resize(levels, k // 32))).repeat(32)
    a = np.empty((k // 512, 16))
    for p in range(k // 512):
        a[p, :8] = np.random.permutation(np.resize(levels, 8))
        for g in range(8):
            far = levels[np.abs(levels - a[p, g]) >= 10]
            a[p, g + 8] = far[np.random.randint(len(far))]
    return np.exp2(a.ravel()).repeat(32)


def f64(x):
    return np.asarray(x).astype(np.float64)


def striped(idx):
    return np.tile(idx.reshape(-1, 16).T, (8, 1)).astype(np.uint16)


def unstriped(offs):
    return offs[:16].T.reshape(-1).astype(np.int64)


E2M1 = np.array([0.0, 0.5, 1.0, 1.5, 2.0, 3.0, 4.0, 6.0, -0.0, -0.5, -1.0, -1.5, -2.0, -3.0, -4.0, -6.0])


def pack_weight(w, fmt):
    k, n = w.shape
    w = f64(np.asarray(w, np.float32).astype(ml_dtypes.bfloat16)).reshape(k // 32, 32, n)
    amax = np.abs(w).max(1)
    if fmt == "e4m3":
        byte = np.frexp(amax)[1] - 1 + 127 - 7
    else:
        mant, ex = np.frexp(amax / 6.0)
        byte = np.where(mant > 0.5, ex, ex - 1) + 127
    byte = np.clip(np.where(amax > 0, byte, 1), 1, 254)
    scaled = (w * np.exp2(127.0 - byte)[:, None, :]).reshape(k, n).astype(np.float32)
    by_word = np.ascontiguousarray(scaled.reshape(k // 512, 128, 4, n).transpose(0, 1, 3, 2))
    if fmt == "e4m3":
        words = by_word.astype(ml_dtypes.float8_e4m3fn).view(np.uint8)
    else:
        c = by_word.astype(ml_dtypes.float4_e2m1fn).view(np.uint8) & 0xF
        words = (c[..., 0::2] | (c[..., 1::2] << 4)).reshape(k // 512, 128, 2 * n)
    return np.ascontiguousarray(words), np.ascontiguousarray(byte.astype(np.uint8).reshape(k // 512, 16, n))


def unpack_weight(words, scales, fmt):
    g, _, n = scales.shape
    words = np.ascontiguousarray(words).reshape(g, 128, n, -1)
    if fmt == "e4m3":
        vals = words.view(ml_dtypes.float8_e4m3fn).astype(np.float64)
    else:
        nib = np.empty((g, 128, n, 4), np.uint8)
        nib[..., 0::2] = words & 0xF
        nib[..., 1::2] = words >> 4
        vals = E2M1[nib]
    vals = vals * np.repeat(np.exp2(scales.astype(np.float64) - 127.0), 8, axis=1)[..., None]
    return vals.transpose(0, 1, 3, 2).reshape(g * 512, n)


def gelu(v):
    return 0.5 * v * (1.0 + np.tanh(np.sqrt(2.0 / np.pi) * (v + 0.044715 * v**3)))


K, T, E, C, H, N = 2560, 768, 2, 256, 512, 512


def by_expert(wq, xq):
    return np.concatenate([wq[e].T @ xq[:, e * C:(e + 1) * C] for e in range(E)], axis=1)


def setup_inputs():
    n = np.random.standard_normal
    s = mx_kscale(K)[:, None]
    u = mx_kscale(H)
    w1 = [pack_weight(m, "e2m1") for m in n((E + 1, K, H)) / np.sqrt(K) / s[None] * u[None, None, :]]
    w2 = [pack_weight(m, "e2m1") for m in n((E + 1, H, N)) / np.sqrt(H) / u[None, :, None]]
    x = pack_weight(n((K, T)) * s, "e4m3")
    return {
        "x_words": x[0],
        "x_scales": x[1],
        "w1_words": np.stack([m[0] for m in w1]),
        "w1_scales": np.stack([m[1] for m in w1]),
        "w2_words": np.stack([m[0] for m in w2]),
        "w2_scales": np.stack([m[1] for m in w2]),
        "gate": np.tile(np.random.uniform(0.2, 1.0, E * C), (N, 1)).astype(np.float32),
        "offs": striped(np.random.permutation(T)[:E * C]),
    }


def reference(x_words, x_scales, w1_words, w1_scales, w2_words, w2_scales, gate, offs):
    idx = unstriped(offs)
    w1 = np.stack([unpack_weight(w1_words[e], w1_scales[e], "e2m1") for e in range(E + 1)])
    w2 = np.stack([unpack_weight(w2_words[e], w2_scales[e], "e2m1") for e in range(E + 1)])
    w1q, w2q = w1, w2
    xs = unpack_weight(x_words, x_scales, "e4m3")
    hs = gelu(w1q[E].T @ xs)
    ys = w2q[E].T @ mxq(hs, 0, "e4m3")
    xq = unpack_weight(x_words, x_scales, "e4m3")[:, idx]
    h = gelu(by_expert(w1q, xq))
    y = by_expert(w2q, mxq(h, 0, "e4m3"))
    out = ys
    out[:, idx] += f64(gate) * y
    return out

@@ -1,0 +1,243 @@
+from contextlib import ExitStack
+
+import concourse.mybir as mybir
+from concourse.masks import make_identity
+
+K, T, E, C, H, N = 2560, 768, 2, 256, 512, 512
+FLOPS = 2 * (E * C + T) * (K * H + H * N)
+
+F32 = mybir.dt.float32
+BF16 = mybir.dt.bfloat16
+I32 = mybir.dt.int32
+U32 = mybir.dt.uint32
+U16 = mybir.dt.uint16
+U8 = mybir.dt.uint8
+FP8X4 = mybir.dt.float8_e4m3fn_x4
+FP4X4 = mybir.dt.float4_e2m1fn_x4
+GELU = mybir.ActivationFunctionType.Gelu_apprx_tanh
+MULT = mybir.AluOpType.mult
+ADD = mybir.AluOpType.add
+
+P = 128
+PASSES = K // 512
+GROUP = 256
+NT = N // P
+SHARED = E
+
+
+def tile_moe_shr_mlp_gelu_kernel(
+    tc, x_words, x_scales, w1_words, w1_scales, w2_words, w2_scales, gate, offs, out
+):
+    nc = tc.nc
+    with ExitStack() as ctx:
+        keep = ctx.enter_context(tc.tile_pool(name="keep", bufs=1))
+        stage = ctx.enter_context(tc.tile_pool(name="stage", bufs=3))
+        acc_pool = ctx.enter_context(tc.psum_pool(name="acc", bufs=3))
+        turn_pool = ctx.enter_context(tc.psum_pool(name="turn", bufs=1))
+        y_pool = ctx.enter_context(tc.psum_pool(name="y", bufs=4))
+
+        def held(shape, dtype, name):
+            return keep.tile(shape, dtype, name=name, align_bytes=64)
+
+        offsets = keep.tile([P, E * C // 16], U16, name="offsets")
+        xw = [held([P, T], I32, "xw%d" % o) for o in range(PASSES)]
+        xs_packed = held([P, T], U8, "xs_packed")
+        xs_mid = held([P, 3, T], U8, "xs_mid")
+        xs_last = held([P, T], U8, "xs_last")
+        w1w = [held([P, PASSES, 2 * H], U8, "w1w%d" % e) for e in range(E + 1)]
+        w1s = [held([P, PASSES, H], U8, "w1s%d" % e) for e in range(E + 1)]
+        w2w = held([P, E + 1, 2 * N], U8, "w2w")
+        w2s = held([P, E + 1, N], U8, "w2s")
+        gates = [held([P, NT, C], F32, "gates%d" % e) for e in range(E)]
+        gw = [held([P, E * C], I32, "gw%d" % o) for o in range(PASSES)]
+        gs_packed = held([P, E * C], U8, "gs_packed")
+        gs_mid = [held([P, E * C], U8, "gs_mid%d" % o) for o in range(3)]
+        gs_last = held([P, E * C], U8, "gs_last")
+        windows = [held([P, T], F32, "window%d" % c) for c in range(NT)]
+        zeros = held([P, 16], F32, "zeros")
+        ident = held([P, P], F32, "ident")
+
+        def zero(tile):
+            nc.vector.memset(tile[:].bitcast(I32), 0)
+
+        def load_planes(queue, tile, rows):
+            by_r = rows.rearrange("s (q r) w -> r q s w", r=4)
+            for r in range(4):
+                queue.dma_start(out=tile[r:P:32, :, :].bitcast(I32), in_=by_r[r].bitcast(I32))
+
+        def load_x(o):
+            nc.sync.dma_start(out=xw[o][:], in_=x_words[o].rearrange("p t r -> p (t r)").bitcast(I32))
+
+        def load_w1(e, lo, hi):
+            nc.sync.dma_start(
+                out=w1w[e][:, lo:hi, :].bitcast(I32),
+                in_=w1_words[e, lo:hi].rearrange("s p b -> p s b").bitcast(I32),
+            )
+
+        def load_w2(lo, hi):
+            nc.sync.dma_start(
+                out=w2w[:, lo:hi, :].bitcast(I32),
+                in_=w2_words[lo:hi, 0].rearrange("e p b -> p e b").bitcast(I32),
+            )
+
+        def load_gate(e, lo, hi):
+            nc.sync.dma_start(
+                out=gates[e][:, lo:hi, :],
+                in_=gate[lo * P : hi * P, e * C : (e + 1) * C].rearrange("(c p) j -> p c j", p=P),
+            )
+
+        nc.gpsimd.memset(zeros[:], 0.0)
+        make_identity(nc, ident[:])
+        for tile in [xs_packed, xs_last, w1s[0]] + gs_mid + [w1s[1], w2s, w1s[2], xs_mid]:
+            zero(tile)
+
+        nc.sync.dma_start(offsets[:], offs)
+        for q in range(4):
+            nc.sync.dma_start(
+                out=xs_packed[32 * q : 32 * q + 16, :].bitcast(I32),
+                in_=x_scales[0:4, 4 * q : 4 * q + 4, :].bitcast(I32),
+            )
+        load_x(0)
+        load_x(1)
+        load_w1(0, 0, PASSES)
+        nc.vector.tensor_copy(gs_packed[:], xs_packed[:].indirect(offsets[:]))
+        for o in range(3):
+            nc.scalar.dma_start(
+                out=gs_mid[o][0:112, :].bitcast(I32),
+                in_=gs_packed[4 * (o + 1) : 4 * (o + 1) + 112, :].bitcast(I32),
+            )
+        last_rows = x_scales[PASSES - 1].rearrange("(q r) t -> r q t", r=4)
+        for r in range(4):
+            nc.gpsimd.dma_start(out=xs_last[r:P:32, :].bitcast(I32), in_=last_rows[r].bitcast(I32))
+        for c in range(NT):
+            nc.scalar.activation(out=windows[c][:], in_=zeros[:, 0:1].to_broadcast([P, T]), func=GELU)
+        load_planes(nc.sync, w1s[0], w1_scales[0])
+        load_x(2)
+        load_x(3)
+        load_x(4)
+        load_planes(nc.sync, w1s[1], w1_scales[1])
+        load_w1(1, 0, PASSES)
+        load_w2(0, 1)
+        load_planes(nc.sync, w2s, w2_scales.rearrange("e s q n -> (e s) q n"))
+        load_gate(0, 0, 2)
+        load_planes(nc.sync, w1s[2], w1_scales[2])
+        load_planes(nc.sync, xs_mid, x_scales[1:4])
+        load_w1(2, 0, 2)
+        load_w1(2, 2, PASSES)
+        load_w2(1, 3)
+        load_gate(0, 2, 4)
+        load_gate(1, 0, 4)
+
+        g_planes = [gs_packed] + gs_mid + [gs_last]
+        x_planes = [xs_packed[:]] + [xs_mid[:, o, :] for o in range(3)] + [xs_last[:]]
+
+        def gather(e):
+            cols = slice(e * C, (e + 1) * C)
+            lst = offsets[:, e * C // 16 : (e + 1) * C // 16]
+            for o in range(PASSES):
+                if o == PASSES - 1:
+                    nc.vector.tensor_copy(gs_last[:, cols], xs_last[:].indirect(lst))
+                nc.vector.tensor_copy(gw[o][:, cols].bitcast(U32), xw[o][:].bitcast(U32).indirect(lst))
+
+        def first_layer(e, words, planes, col0, pass_major):
+            accs = [acc_pool.tile([P, H], F32, name="acc") for j in range(2)]
+            order = [(o, j) for o in range(PASSES) for j in range(2)]
+            if not pass_major:
+                order = [(o, j) for j in range(2) for o in range(PASSES)]
+            for o, j in order:
+                cols = slice(col0 + j * P, col0 + (j + 1) * P)
+                nc.tensor.matmul_mx(
+                    out=accs[j][:],
+                    lhsT=words[o][:, cols].bitcast(FP8X4),
+                    lhsT_scale=planes[o][:, cols],
+                    rhs=w1w[e][:, o, :].bitcast(FP4X4),
+                    rhs_scale=w1s[e][:, o, :],
+                    start=(o == 0),
+                    stop=(o == PASSES - 1),
+                )
+            return accs
+
+        def turn(accs):
+            turned = turn_pool.tile([P, 2, 2, P], F32, name="turned")
+            for j in range(2):
+                h = stage.tile([P, H], BF16, name="h", align_bytes=64)
+                nc.scalar.activation(
+                    out=h[:].rearrange("q (u p d) -> q u p d", u=2, d=2),
+                    in_=accs[j][:].rearrange("q (p u d) -> q u p d", u=2, d=2),
+                    func=GELU,
+                )
+                pairs = h[:].bitcast(F32)
+                for u in range(2):
+                    nc.tensor.transpose(turned[:, j, u, :], pairs[:, u * P : (u + 1) * P], ident[:])
+            grouped = stage.tile([P, 4 * GROUP], BF16, name="grouped", align_bytes=64)
+            nc.scalar.copy(
+                out=grouped[:].bitcast(F32).rearrange("p (j t u) -> p j t u", j=2, u=2),
+                in_=turned[:].rearrange("p j u t -> p j t u"),
+            )
+            return grouped
+
+        def quantise(grouped, codes, scales):
+            nc.vector.quantize_mx(out=codes.bitcast(FP8X4), scales=scales, in_=grouped[:])
+
+        def second_layer(e, c, dst, codes, scales):
+            nc.tensor.matmul_mx(
+                out=dst,
+                lhsT=w2w[:, e, 2 * c * P : 2 * (c + 1) * P].bitcast(FP4X4),
+                lhsT_scale=w2s[:, e, c * P : (c + 1) * P],
+                rhs=codes.bitcast(FP8X4),
+                rhs_scale=scales,
+                start=True,
+                stop=True,
+            )
+
+        def scatter(e, c):
+            lst = offsets[:, e * C // 16 : (e + 1) * C // 16]
+            nc.vector.tensor_copy(windows[c][:].indirect(lst), gated[e][:, c, :])
+
+        for e in range(E):
+            gather(e)
+        gated = []
+        for e in range(E):
+            accs = first_layer(e, [t[:] for t in gw], [t[:] for t in g_planes], e * C, True)
+            grouped = turn(accs)
+            codes = held([P, C], U32, "codes%d" % e)
+            scales = held([P, C], U8, "scales%d" % e)
+            quantise(grouped, codes[:], scales[:])
+            yg = held([P, NT, C], F32, "gated%d" % e)
+            for b in range(2):
+                bank = y_pool.tile([P, 2, C], F32, name="y")
+                for i in range(2):
+                    second_layer(e, 2 * b + i, bank[:, i, :], codes[:], scales[:])
+                nc.vector.tensor_tensor(yg[:, 2 * b : 2 * b + 2, :], bank[:], gates[e][:, 2 * b : 2 * b + 2, :], MULT)
+            gated.append(yg)
+
+        s_codes = held([P, T], U32, "s_codes")
+        s_scales = held([P, T], U8, "s_scales")
+        for g in range(T // GROUP):
+            cols = slice(g * GROUP, (g + 1) * GROUP)
+            accs = first_layer(SHARED, [t[:] for t in xw], x_planes, g * GROUP, g == 0)
+            quantise(turn(accs), s_codes[:, cols], s_scales[:, cols])
+        wide = slice(0, 2 * GROUP)
+        rest = slice(2 * GROUP, T)
+        ys_wide = []
+        for c in range(NT):
+            bank = y_pool.tile([P, 2 * GROUP], F32, name="y")
+            second_layer(SHARED, c, bank[:], s_codes[:, wide], s_scales[:, wide])
+            ys_wide.append(bank[:])
+        ys_rest = []
+        for b in range(2):
+            bank = acc_pool.tile([P, 2, GROUP], F32, name="acc")
+            for i in range(2):
+                second_layer(SHARED, 2 * b + i, bank[:, i, :], s_codes[:, rest], s_scales[:, rest])
+                ys_rest.append(bank[:, i, :])
+
+        for c in range(NT):
+            scatter(0, c)
+        res = [held([P, T], F32, "res%d" % c) for c in range(NT)]
+        for c in range(NT):
+            scatter(1, c)
+            nc.vector.tensor_tensor(res[c][:, wide], ys_wide[c], windows[c][:, wide], ADD)
+            nc.sync.dma_start(out=out[c * P : (c + 1) * P, wide], in_=res[c][:, wide])
+        for c in range(NT):
+            nc.vector.tensor_tensor(res[c][:, rest], ys_rest[c], windows[c][:, rest], ADD)
+            nc.sync.dma_start(out=out[c * P : (c + 1) * P, rest], in_=res[c][:, rest])

@@ -23,6 +23,8 @@ PASSES = K // 512
 GROUP = 256
 NT = N // P
 SHARED = E
+EARLY = 3
+EDGE = 16
 
 
 def tile_moe_shr_mlp_gelu_kernel(
@@ -36,25 +38,17 @@ def tile_moe_shr_mlp_gelu_kernel(
         turn_pool = ctx.enter_context(tc.psum_pool(name="turn", bufs=1))
         y_pool = ctx.enter_context(tc.psum_pool(name="y", bufs=4))
 
-        def held(shape, dtype, name):
-            return keep.tile(shape, dtype, name=name, align_bytes=64)
+        def held(shape, dtype, name, tag=None):
+            return keep.tile(shape, dtype, name=name, tag=tag or name, align_bytes=64)
 
         offsets = keep.tile([P, E * C // 16], U16, name="offsets")
-        xw = [held([P, T], I32, "xw%d" % o) for o in range(PASSES)]
-        xs_packed = held([P, T], U8, "xs_packed")
-        xs_mid = held([P, 3, T], U8, "xs_mid")
-        xs_last = held([P, T], U8, "xs_last")
-        w1w = [held([P, PASSES, 2 * H], U8, "w1w%d" % e) for e in range(E + 1)]
+        x_early = held([P, EARLY, T], I32, "x_early")
+        xs = held([P, PASSES, T], U8, "xs")
         w1s = [held([P, PASSES, H], U8, "w1s%d" % e) for e in range(E + 1)]
-        w2w = held([P, E + 1, 2 * N], U8, "w2w")
         w2s = held([P, E + 1, N], U8, "w2s")
-        gates = [held([P, NT, C], F32, "gates%d" % e) for e in range(E)]
-        gw = [held([P, E * C], I32, "gw%d" % o) for o in range(PASSES)]
-        gs_packed = held([P, E * C], U8, "gs_packed")
-        gs_mid = [held([P, E * C], U8, "gs_mid%d" % o) for o in range(3)]
-        gs_last = held([P, E * C], U8, "gs_last")
         windows = [held([P, T], F32, "window%d" % c) for c in range(NT)]
-        zeros = held([P, 16], F32, "zeros")
+        zeros = [held([P, EDGE], F32, "zero%d" % z, "slot%d" % z) for z in range(4)]
+        zero_col = held([P, 1], F32, "zero_col")
         ident = held([P, P], F32, "ident")
 
         def zero(tile):
@@ -65,79 +59,69 @@ def tile_moe_shr_mlp_gelu_kernel(
             for r in range(4):
                 queue.dma_start(out=tile[r:P:32, :, :].bitcast(I32), in_=by_r[r].bitcast(I32))
 
-        def load_x(o):
-            nc.sync.dma_start(out=xw[o][:], in_=x_words[o].rearrange("p t r -> p (t r)").bitcast(I32))
+        def load_x(dst, o):
+            nc.sync.dma_start(out=dst, in_=x_words[o].rearrange("p t r -> p (t r)").bitcast(I32))
 
-        def load_w1(e, lo, hi):
+        def load_words(dst, words):
+            nc.sync.dma_start(out=dst.bitcast(I32), in_=words.rearrange("s p b -> p s b").bitcast(I32))
+
+        def load_gate(dst, e, lo, hi):
             nc.sync.dma_start(
-                out=w1w[e][:, lo:hi, :].bitcast(I32),
-                in_=w1_words[e, lo:hi].rearrange("s p b -> p s b").bitcast(I32),
+                out=dst, in_=gate[lo * P : hi * P, e * C : (e + 1) * C].rearrange("(c p) j -> p c j", p=P)
             )
 
-        def load_w2(lo, hi):
-            nc.sync.dma_start(
-                out=w2w[:, lo:hi, :].bitcast(I32),
-                in_=w2_words[lo:hi, 0].rearrange("e p b -> p e b").bitcast(I32),
-            )
+        nc.gpsimd.memset(zero_col[:], 0.0)
+        for z in range(4):
+            nc.gpsimd.memset(zeros[z][:], 0.0)
 
-        def load_gate(e, lo, hi):
-            nc.sync.dma_start(
-                out=gates[e][:, lo:hi, :],
-                in_=gate[lo * P : hi * P, e * C : (e + 1) * C].rearrange("(c p) j -> p c j", p=P),
-            )
+        def free_slot(z):
+            nc.vector.tensor_copy(windows[z][:, 0:EDGE], zeros[z][:])
 
-        nc.gpsimd.memset(zeros[:], 0.0)
+        zero(xs)
+        zero(w1s[0])
+        free_slot(0)
+        free_slot(1)
+        zero(w1s[SHARED])
+        free_slot(2)
+        zero(w2s)
+        zero(w1s[1])
+        free_slot(3)
+        for c in range(NT):
+            nc.scalar.activation(out=windows[c][:, EDGE:T], in_=zero_col[:].to_broadcast([P, T - EDGE]), func=GELU)
         make_identity(nc, ident[:])
-        for tile in [xs_packed, xs_last, w1s[0]] + gs_mid + [w1s[1], w2s, w1s[2], xs_mid]:
-            zero(tile)
 
         nc.sync.dma_start(offsets[:], offs)
-        for q in range(4):
-            nc.sync.dma_start(
-                out=xs_packed[32 * q : 32 * q + 16, :].bitcast(I32),
-                in_=x_scales[0:4, 4 * q : 4 * q + 4, :].bitcast(I32),
-            )
-        load_x(0)
-        load_x(1)
-        load_w1(0, 0, PASSES)
-        nc.vector.tensor_copy(gs_packed[:], xs_packed[:].indirect(offsets[:]))
-        for o in range(3):
-            nc.scalar.dma_start(
-                out=gs_mid[o][0:112, :].bitcast(I32),
-                in_=gs_packed[4 * (o + 1) : 4 * (o + 1) + 112, :].bitcast(I32),
-            )
-        last_rows = x_scales[PASSES - 1].rearrange("(q r) t -> r q t", r=4)
-        for r in range(4):
-            nc.gpsimd.dma_start(out=xs_last[r:P:32, :].bitcast(I32), in_=last_rows[r].bitcast(I32))
-        for c in range(NT):
-            nc.scalar.activation(out=windows[c][:], in_=zeros[:, 0:1].to_broadcast([P, T]), func=GELU)
+        for o in range(EARLY):
+            load_x(x_early[:, o, :], o)
+        load_planes(nc.sync, xs, x_scales)
         load_planes(nc.sync, w1s[0], w1_scales[0])
-        load_x(2)
-        load_x(3)
-        load_x(4)
-        load_planes(nc.sync, w1s[1], w1_scales[1])
-        load_w1(1, 0, PASSES)
-        load_w2(0, 1)
+        w1_first = held([P, PASSES, 2 * H], U8, "w1_first", "slot0")
+        load_words(w1_first[:], w1_words[0])
+        x_late = held([P, PASSES - EARLY, T], I32, "x_late", "slot1")
+        for o in range(EARLY, PASSES):
+            load_x(x_late[:, o - EARLY, :], o)
+        xw = [x_early[:, o, :] for o in range(EARLY)] + [x_late[:, o, :] for o in range(PASSES - EARLY)]
+        load_planes(nc.sync, w1s[SHARED], w1_scales[SHARED])
+        w_shared = held([P, PASSES + E + 1, 2 * H], U8, "w_shared", "slot2")
+        w2w = w_shared[:, PASSES:, :]
+        load_words(w2w, w2_words[:, 0])
+        load_words(w_shared[:, 0:2, :], w1_words[SHARED, 0:2])
+        load_words(w_shared[:, 2:PASSES, :], w1_words[SHARED, 2:PASSES])
         load_planes(nc.sync, w2s, w2_scales.rearrange("e s q n -> (e s) q n"))
-        load_gate(0, 0, 2)
-        load_planes(nc.sync, w1s[2], w1_scales[2])
-        load_planes(nc.sync, xs_mid, x_scales[1:4])
-        load_w1(2, 0, 2)
-        load_w1(2, 2, PASSES)
-        load_w2(1, 3)
-        load_gate(0, 2, 4)
-        load_gate(1, 0, 4)
+        load_planes(nc.sync, w1s[1], w1_scales[1])
+        w1_second = held([P, PASSES, 2 * H], U8, "w1_second", "slot3")
+        load_words(w1_second[:], w1_words[1])
+        w1w = [w1_first[:], w1_second[:], w_shared[:, 0:PASSES, :]]
+        x_planes = [xs[:, o, :] for o in range(PASSES)]
 
-        g_planes = [gs_packed] + gs_mid + [gs_last]
-        x_planes = [xs_packed[:]] + [xs_mid[:, o, :] for o in range(3)] + [xs_last[:]]
+        def slots_of(e):
+            return offsets[:, e * C // 16 : (e + 1) * C // 16]
 
-        def gather(e):
-            cols = slice(e * C, (e + 1) * C)
-            lst = offsets[:, e * C // 16 : (e + 1) * C // 16]
-            for o in range(PASSES):
-                if o == PASSES - 1:
-                    nc.vector.tensor_copy(gs_last[:, cols], xs_last[:].indirect(lst))
-                nc.vector.tensor_copy(gw[o][:, cols].bitcast(U32), xw[o][:].bitcast(U32).indirect(lst))
+        def gather_words(e, o, dst):
+            nc.vector.tensor_copy(dst.bitcast(U32), xw[o].bitcast(U32).indirect(slots_of(e)))
+
+        def gather_scales(e, o, dst):
+            nc.vector.tensor_copy(dst, x_planes[o].indirect(slots_of(e)))
 
         def first_layer(e, words, planes, col0, pass_major):
             accs = [acc_pool.tile([P, H], F32, name="acc") for j in range(2)]
@@ -157,7 +141,7 @@ def tile_moe_shr_mlp_gelu_kernel(
                 )
             return accs
 
-        def turn(accs):
+        def turn(accs, grouped):
             turned = turn_pool.tile([P, 2, 2, P], F32, name="turned")
             for j in range(2):
                 h = stage.tile([P, H], BF16, name="h", align_bytes=64)
@@ -169,7 +153,6 @@ def tile_moe_shr_mlp_gelu_kernel(
                 pairs = h[:].bitcast(F32)
                 for u in range(2):
                     nc.tensor.transpose(turned[:, j, u, :], pairs[:, u * P : (u + 1) * P], ident[:])
-            grouped = stage.tile([P, 4 * GROUP], BF16, name="grouped", align_bytes=64)
             nc.scalar.copy(
                 out=grouped[:].bitcast(F32).rearrange("p (j t u) -> p j t u", j=2, u=2),
                 in_=turned[:].rearrange("p j u t -> p j t u"),
@@ -192,31 +175,65 @@ def tile_moe_shr_mlp_gelu_kernel(
 
         def scatter(e, c):
             lst = offsets[:, e * C // 16 : (e + 1) * C // 16]
-            nc.vector.tensor_copy(windows[c][:].indirect(lst), gated[e][:, c, :])
+            nc.vector.tensor_tensor(windows[c][:].indirect(lst), y_slots[e, c], gates[:, e, c, :], MULT)
 
-        for e in range(E):
-            gather(e)
-        gated = []
-        for e in range(E):
-            accs = first_layer(e, [t[:] for t in gw], [t[:] for t in g_planes], e * C, True)
-            grouped = turn(accs)
+        y_slots = {}
+
+        def routed(e, accs):
+            grouped = turn(accs, held([P, 4 * C], BF16, "grouped_routed%d" % e))
             codes = held([P, C], U32, "codes%d" % e)
             scales = held([P, C], U8, "scales%d" % e)
             quantise(grouped, codes[:], scales[:])
-            yg = held([P, NT, C], F32, "gated%d" % e)
-            for b in range(2):
-                bank = y_pool.tile([P, 2, C], F32, name="y")
-                for i in range(2):
-                    second_layer(e, 2 * b + i, bank[:, i, :], codes[:], scales[:])
-                nc.vector.tensor_tensor(yg[:, 2 * b : 2 * b + 2, :], bank[:], gates[e][:, 2 * b : 2 * b + 2, :], MULT)
-            gated.append(yg)
+            banks = [y_pool.tile([P, 2, C], F32, name="y") for b in range(2)]
+            for c in range(NT):
+                second_layer(e, c, banks[c // 2][:, c % 2, :], codes[:], scales[:])
+            return banks
+
+        def unload(e, b, bank, tag):
+            y = held([P, 2, C], F32, "y_slots%d_%d" % (e, b), tag)
+            nc.scalar.copy(out=y[:], in_=bank[:])
+            for i in range(2):
+                y_slots[e, 2 * b + i] = y[:, i, :]
 
         s_codes = held([P, T], U32, "s_codes")
         s_scales = held([P, T], U8, "s_scales")
-        for g in range(T // GROUP):
+
+        def shared_front(g):
             cols = slice(g * GROUP, (g + 1) * GROUP)
-            accs = first_layer(SHARED, [t[:] for t in xw], x_planes, g * GROUP, g == 0)
-            quantise(turn(accs), s_codes[:, cols], s_scales[:, cols])
+            accs = first_layer(SHARED, xw, x_planes, g * GROUP, g == 0)
+            grouped = turn(accs, held([P, 4 * GROUP], BF16, "grouped_shared%d" % g))
+            quantise(grouped, s_codes[:, cols], s_scales[:, cols])
+
+        words0 = [held([P, C], I32, "words0_%d" % o)[:] for o in range(PASSES)]
+        planes0 = [held([P, C], U8, "planes0_%d" % o)[:] for o in range(PASSES)]
+        for o in range(EARLY):
+            gather_words(0, o, words0[o])
+        for o in range(PASSES):
+            gather_scales(0, o, planes0[o])
+        for o in range(EARLY, PASSES):
+            gather_words(0, o, words0[o])
+        accs = first_layer(0, words0, planes0, 0, True)
+        gates = held([P, E, NT, C], F32, "gates", "slot0")
+        load_gate(gates[:, 0, 0:2, :], 0, 0, 2)
+        load_gate(gates[:, 0, 2:4, :], 0, 2, 4)
+        load_gate(gates[:, 1, :, :], 1, 0, 4)
+        banks0 = routed(0, accs)
+        unload(0, 0, banks0[0], None)
+        words1_early = held([P, EARLY, C], I32, "words1_early", "words0_2")
+        planes1_all = held([P, PASSES, C], U8, "planes1", "planes0_2")
+        words1_late = held([P, PASSES - EARLY, C], I32, "words1_late", "grouped_routed0")
+        words1 = [words1_early[:, o, :] for o in range(EARLY)] + [words1_late[:, o, :] for o in range(PASSES - EARLY)]
+        planes1 = [planes1_all[:, o, :] for o in range(PASSES)]
+        for o in range(PASSES):
+            gather_scales(1, o, planes1[o])
+            gather_words(1, o, words1[o])
+        shared_front(0)
+        banks1 = routed(1, first_layer(1, words1, planes1, 0, True))
+        unload(0, 1, banks0[1], "grouped_routed1")
+        shared_front(1)
+        unload(1, 0, banks1[0], "grouped_shared1")
+        shared_front(2)
+        unload(1, 1, banks1[1], "grouped_shared2")
         wide = slice(0, 2 * GROUP)
         rest = slice(2 * GROUP, T)
         ys_wide = []
@@ -238,6 +255,5 @@ def tile_moe_shr_mlp_gelu_kernel(
             scatter(1, c)
             nc.vector.tensor_tensor(res[c][:, wide], ys_wide[c], windows[c][:, wide], ADD)
             nc.sync.dma_start(out=out[c * P : (c + 1) * P, wide], in_=res[c][:, wide])
-        for c in range(NT):
             nc.vector.tensor_tensor(res[c][:, rest], ys_rest[c], windows[c][:, rest], ADD)
             nc.sync.dma_start(out=out[c * P : (c + 1) * P, rest], in_=res[c][:, rest])

@@ -44,71 +44,69 @@ def tile_moe_shr_mlp_gelu_kernel(
         offsets = keep.tile([P, E * C // 16], U16, name="offsets")
         x_early = held([P, EARLY, T], I32, "x_early")
         xs = held([P, PASSES, T], U8, "xs")
-        w1s = [held([P, PASSES, H], U8, "w1s%d" % e) for e in range(E + 1)]
+        w1s_first = held([P, PASSES, H], U8, "w1s_first")
+        w1s_rest = held([P, E * PASSES, H], U8, "w1s_rest")
+        w1s = [w1s_first[:], w1s_rest[:, 0:PASSES, :], w1s_rest[:, PASSES:, :]]
         w2s = held([P, E + 1, N], U8, "w2s")
         windows = [held([P, T], F32, "window%d" % c) for c in range(NT)]
-        zeros = [held([P, EDGE], F32, "zero%d" % z, "slot%d" % z) for z in range(4)]
+        zeros = [held([P, EDGE], F32, "zero%d" % z, "slot%d" % z) for z in range(5)]
         zero_col = held([P, 1], F32, "zero_col")
         ident = held([P, P], F32, "ident")
 
-        def zero(tile):
-            nc.vector.memset(tile[:].bitcast(I32), 0)
+        def zero(engine, tile):
+            engine.memset(tile[:].bitcast(I32), 0)
 
         def load_planes(queue, tile, rows):
             by_r = rows.rearrange("s (q r) w -> r q s w", r=4)
             for r in range(4):
                 queue.dma_start(out=tile[r:P:32, :, :].bitcast(I32), in_=by_r[r].bitcast(I32))
 
-        def load_x(dst, o):
-            nc.sync.dma_start(out=dst, in_=x_words[o].rearrange("p t r -> p (t r)").bitcast(I32))
+        def load_x(dst, lo, hi):
+            nc.sync.dma_start(out=dst, in_=x_words[lo:hi].rearrange("o p t r -> p o (t r)").bitcast(I32))
 
         def load_words(dst, words):
             nc.sync.dma_start(out=dst.bitcast(I32), in_=words.rearrange("s p b -> p s b").bitcast(I32))
 
-        def load_gate(dst, e, lo, hi):
-            nc.sync.dma_start(
-                out=dst, in_=gate[lo * P : hi * P, e * C : (e + 1) * C].rearrange("(c p) j -> p c j", p=P)
-            )
+        def load_gate(dst, rows, cols):
+            nc.sync.dma_start(out=dst, in_=gate[rows, cols].rearrange("(c p) j -> p c j", p=P))
 
         nc.gpsimd.memset(zero_col[:], 0.0)
-        for z in range(4):
+        for z in range(5):
             nc.gpsimd.memset(zeros[z][:], 0.0)
 
-        def free_slot(z):
-            nc.vector.tensor_copy(windows[z][:, 0:EDGE], zeros[z][:])
+        def free_slot(engine, z):
+            engine.tensor_copy(windows[z % 2][:, z // 2 * EDGE : (z // 2 + 1) * EDGE], zeros[z][:])
 
-        zero(xs)
-        zero(w1s[0])
-        free_slot(0)
-        free_slot(1)
-        zero(w1s[SHARED])
-        free_slot(2)
-        zero(w2s)
-        zero(w1s[1])
-        free_slot(3)
-        for c in range(NT):
-            nc.scalar.activation(out=windows[c][:, EDGE:T], in_=zero_col[:].to_broadcast([P, T - EDGE]), func=GELU)
         make_identity(nc, ident[:])
+        zero(nc.vector, xs)
+        free_slot(nc.vector, 0)
+        free_slot(nc.vector, 1)
+        zero(nc.vector, w1s_first)
+        zero(nc.vector, w2s)
+        zero(nc.vector, w1s_rest)
+        for z in (2, 4, 3):
+            free_slot(nc.vector, z)
+        for c, first in enumerate([3 * EDGE, 2 * EDGE, 0, 0]):
+            nc.scalar.activation(out=windows[c][:, first:T], in_=zero_col[:].to_broadcast([P, T - first]), func=GELU)
 
         nc.sync.dma_start(offsets[:], offs)
-        for o in range(EARLY):
-            load_x(x_early[:, o, :], o)
+        load_x(x_early[:, 0:1, :], 0, 1)
+        load_x(x_early[:, 1:EARLY, :], 1, EARLY)
         load_planes(nc.sync, xs, x_scales)
-        load_planes(nc.sync, w1s[0], w1_scales[0])
+        load_planes(nc.gpsimd, w2s, w2_scales.rearrange("e s q n -> (e s) q n"))
         w1_first = held([P, PASSES, 2 * H], U8, "w1_first", "slot0")
         load_words(w1_first[:], w1_words[0])
         x_late = held([P, PASSES - EARLY, T], I32, "x_late", "slot1")
-        for o in range(EARLY, PASSES):
-            load_x(x_late[:, o - EARLY, :], o)
+        load_x(x_late[:], EARLY, PASSES)
+        load_planes(nc.sync, w1s_first, w1_scales[0])
         xw = [x_early[:, o, :] for o in range(EARLY)] + [x_late[:, o, :] for o in range(PASSES - EARLY)]
-        load_planes(nc.sync, w1s[SHARED], w1_scales[SHARED])
+        load_planes(nc.sync, w1s_rest, w1_scales[1:].rearrange("e s q i -> (e s) q i"))
         w_shared = held([P, PASSES + E + 1, 2 * H], U8, "w_shared", "slot2")
         w2w = w_shared[:, PASSES:, :]
+        load_words(w_shared[:, 0:PASSES, :], w1_words[SHARED])
         load_words(w2w, w2_words[:, 0])
-        load_words(w_shared[:, 0:2, :], w1_words[SHARED, 0:2])
-        load_words(w_shared[:, 2:PASSES, :], w1_words[SHARED, 2:PASSES])
-        load_planes(nc.sync, w2s, w2_scales.rearrange("e s q n -> (e s) q n"))
-        load_planes(nc.sync, w1s[1], w1_scales[1])
+        gate_first = held([P, 2, C], F32, "gate_first", "slot4")
+        load_gate(gate_first[:], slice(0, 2 * P), slice(0, C))
         w1_second = held([P, PASSES, 2 * H], U8, "w1_second", "slot3")
         load_words(w1_second[:], w1_words[1])
         w1w = [w1_first[:], w1_second[:], w_shared[:, 0:PASSES, :]]
@@ -173,87 +171,108 @@ def tile_moe_shr_mlp_gelu_kernel(
                 stop=True,
             )
 
-        def scatter(e, c):
-            lst = offsets[:, e * C // 16 : (e + 1) * C // 16]
-            nc.vector.tensor_tensor(windows[c][:].indirect(lst), y_slots[e, c], gates[:, e, c, :], MULT)
-
         y_slots = {}
 
-        def routed(e, accs):
-            grouped = turn(accs, held([P, 4 * C], BF16, "grouped_routed%d" % e))
-            codes = held([P, C], U32, "codes%d" % e)
+        def routed_second(e, grouped, tag):
+            codes = held([P, C], U32, "codes%d" % e, tag)
             scales = held([P, C], U8, "scales%d" % e)
             quantise(grouped, codes[:], scales[:])
-            banks = [y_pool.tile([P, 2, C], F32, name="y") for b in range(2)]
-            for c in range(NT):
-                second_layer(e, c, banks[c // 2][:, c % 2, :], codes[:], scales[:])
-            return banks
+            for b in range(2):
+                bank = y_pool.tile([P, 2, C], F32, name="y")
+                for i in range(2):
+                    second_layer(e, 2 * b + i, bank[:, i, :], codes[:], scales[:])
+                y = held([P, 2, C], F32, "y_slots%d_%d" % (e, b))
+                nc.scalar.copy(out=y[:], in_=bank[:])
+                for i in range(2):
+                    y_slots[e, 2 * b + i] = y[:, i, :]
 
-        def unload(e, b, bank, tag):
-            y = held([P, 2, C], F32, "y_slots%d_%d" % (e, b), tag)
-            nc.scalar.copy(out=y[:], in_=bank[:])
-            for i in range(2):
-                y_slots[e, 2 * b + i] = y[:, i, :]
+        def scatter(e, c):
+            nc.vector.tensor_tensor(windows[c][:].indirect(slots_of(e)), y_slots[e, c], gates[e, c], MULT)
 
-        s_codes = held([P, T], U32, "s_codes")
-        s_scales = held([P, T], U8, "s_scales")
+        def shared_first(g):
+            return first_layer(SHARED, xw, x_planes, g * GROUP, False)
 
-        def shared_front(g):
-            cols = slice(g * GROUP, (g + 1) * GROUP)
-            accs = first_layer(SHARED, xw, x_planes, g * GROUP, g == 0)
-            grouped = turn(accs, held([P, 4 * GROUP], BF16, "grouped_shared%d" % g))
-            quantise(grouped, s_codes[:, cols], s_scales[:, cols])
+        def shared_turn(g, accs):
+            return turn(accs, held([P, 4 * GROUP], BF16, "grouped_shared%d" % g))
 
-        words0 = [held([P, C], I32, "words0_%d" % o)[:] for o in range(PASSES)]
+        words_both = [held([P, E * C], I32, "words_both%d" % o) for o in range(EARLY)]
+        words0 = [t[:, 0:C] for t in words_both] + [held([P, C], I32, "words0_%d" % o)[:] for o in range(EARLY, PASSES)]
         planes0 = [held([P, C], U8, "planes0_%d" % o)[:] for o in range(PASSES)]
         for o in range(EARLY):
-            gather_words(0, o, words0[o])
+            nc.vector.tensor_copy(words_both[o][:].bitcast(U32), xw[o].bitcast(U32).indirect(offsets[:]))
         for o in range(PASSES):
             gather_scales(0, o, planes0[o])
         for o in range(EARLY, PASSES):
             gather_words(0, o, words0[o])
         accs = first_layer(0, words0, planes0, 0, True)
-        gates = held([P, E, NT, C], F32, "gates", "slot0")
-        load_gate(gates[:, 0, 0:2, :], 0, 0, 2)
-        load_gate(gates[:, 0, 2:4, :], 0, 2, 4)
-        load_gate(gates[:, 1, :, :], 1, 0, 4)
-        banks0 = routed(0, accs)
-        unload(0, 0, banks0[0], None)
-        words1_early = held([P, EARLY, C], I32, "words1_early", "words0_2")
+        routed_second(0, turn(accs, held([P, 4 * C], BF16, "grouped_routed0")), None)
         planes1_all = held([P, PASSES, C], U8, "planes1", "planes0_2")
         words1_late = held([P, PASSES - EARLY, C], I32, "words1_late", "grouped_routed0")
-        words1 = [words1_early[:, o, :] for o in range(EARLY)] + [words1_late[:, o, :] for o in range(PASSES - EARLY)]
+        words1 = [t[:, C : E * C] for t in words_both] + [words1_late[:, o, :] for o in range(PASSES - EARLY)]
         planes1 = [planes1_all[:, o, :] for o in range(PASSES)]
         for o in range(PASSES):
             gather_scales(1, o, planes1[o])
+        for o in range(EARLY, PASSES):
             gather_words(1, o, words1[o])
-        shared_front(0)
-        banks1 = routed(1, first_layer(1, words1, planes1, 0, True))
-        unload(0, 1, banks0[1], "grouped_routed1")
-        shared_front(1)
-        unload(1, 0, banks1[0], "grouped_shared1")
-        shared_front(2)
-        unload(1, 1, banks1[1], "grouped_shared2")
+        gate_tiles = [gate_first]
+        for name, tag, rows, cols in [
+            ("gate_b", "slot0", slice(2 * P, 4 * P), slice(0, C)),
+            ("gate_c", "words0_3", slice(0, 2 * P), slice(C, E * C)),
+            ("gate_d", "words0_4", slice(2 * P, 4 * P), slice(C, E * C)),
+        ]:
+            tile = held([P, 2, C], F32, name, tag)
+            load_gate(tile[:], rows, cols)
+            gate_tiles.append(tile)
+        gates = {}
+        for e in range(E):
+            for c in range(NT):
+                gates[e, c] = gate_tiles[2 * e + c // 2][:, c % 2, :]
+
+        grouped_s0 = shared_turn(0, shared_first(0))
+        grouped_e1 = turn(first_layer(1, words1, planes1, 0, True), held([P, 4 * C], BF16, "grouped_routed1"))
+        accs_s1 = shared_first(1)
+        scatter(0, 0)
+        scatter(0, 1)
+        scatter(0, 2)
+        routed_second(1, grouped_e1, "y_slots0_0")
+        scatter(0, 3)
+        grouped_s1 = shared_turn(1, accs_s1)
+        accs_s2 = shared_first(2)
+        grouped_s2 = shared_turn(2, accs_s2)
+        scatter(1, 0)
         wide = slice(0, 2 * GROUP)
         rest = slice(2 * GROUP, T)
+        codes_wide = held([P, 2 * GROUP], U32, "codes_wide", "y_slots0_1")
+        scales_wide = held([P, 2 * GROUP], U8, "scales_wide")
+        for g, grouped in enumerate([grouped_s0, grouped_s1]):
+            cols = slice(g * GROUP, (g + 1) * GROUP)
+            quantise(grouped, codes_wide[:, cols], scales_wide[:, cols])
         ys_wide = []
         for c in range(NT):
             bank = y_pool.tile([P, 2 * GROUP], F32, name="y")
-            second_layer(SHARED, c, bank[:], s_codes[:, wide], s_scales[:, wide])
+            second_layer(SHARED, c, bank[:], codes_wide[:], scales_wide[:])
             ys_wide.append(bank[:])
+        scatter(1, 1)
+        scatter(1, 2)
+        codes_rest = held([P, GROUP], U32, "codes_rest", "y_slots1_0")
+        scales_rest = held([P, GROUP], U8, "scales_rest")
+        quantise(grouped_s2, codes_rest[:], scales_rest[:])
         ys_rest = []
         for b in range(2):
             bank = acc_pool.tile([P, 2, GROUP], F32, name="acc")
             for i in range(2):
-                second_layer(SHARED, 2 * b + i, bank[:, i, :], s_codes[:, rest], s_scales[:, rest])
+                second_layer(SHARED, 2 * b + i, bank[:, i, :], codes_rest[:], scales_rest[:])
                 ys_rest.append(bank[:, i, :])
-
-        for c in range(NT):
-            scatter(0, c)
         res = [held([P, T], F32, "res%d" % c) for c in range(NT)]
-        for c in range(NT):
-            scatter(1, c)
-            nc.vector.tensor_tensor(res[c][:, wide], ys_wide[c], windows[c][:, wide], ADD)
-            nc.sync.dma_start(out=out[c * P : (c + 1) * P, wide], in_=res[c][:, wide])
-            nc.vector.tensor_tensor(res[c][:, rest], ys_rest[c], windows[c][:, rest], ADD)
-            nc.sync.dma_start(out=out[c * P : (c + 1) * P, rest], in_=res[c][:, rest])
+
+        def finish(c, cols, ys):
+            nc.vector.tensor_tensor(res[c][:, cols], ys, windows[c][:, cols], ADD)
+            nc.sync.dma_start(out=out[c * P : (c + 1) * P, cols], in_=res[c][:, cols])
+
+        for c in range(NT - 1):
+            finish(c, wide, ys_wide[c])
+        for c in range(NT - 1):
+            finish(c, rest, ys_rest[c])
+        scatter(1, NT - 1)
+        finish(NT - 1, wide, ys_wide[NT - 1])
+        finish(NT - 1, rest, ys_rest[NT - 1])

from contextlib import ExitStack

import concourse.mybir as mybir
from concourse.masks import make_identity

K, T, E, C, H, N = 2560, 768, 2, 256, 512, 512
FLOPS = 2 * (E * C + T) * (K * H + H * N)

F32 = mybir.dt.float32
BF16 = mybir.dt.bfloat16
I32 = mybir.dt.int32
U32 = mybir.dt.uint32
U16 = mybir.dt.uint16
U8 = mybir.dt.uint8
FP8X4 = mybir.dt.float8_e4m3fn_x4
FP4X4 = mybir.dt.float4_e2m1fn_x4
GELU = mybir.ActivationFunctionType.Gelu_apprx_tanh
MULT = mybir.AluOpType.mult
ADD = mybir.AluOpType.add

P = 128
PASSES = K // 512
GROUP = 256
NT = N // P
SHARED = E
EARLY = 3
EDGE = 16


def tile_moe_shr_mlp_gelu_kernel(
    tc, x_words, x_scales, w1_words, w1_scales, w2_words, w2_scales, gate, offs, out
):
    nc = tc.nc
    with ExitStack() as ctx:
        keep = ctx.enter_context(tc.tile_pool(name="keep", bufs=1))
        stage = ctx.enter_context(tc.tile_pool(name="stage", bufs=3))
        acc_pool = ctx.enter_context(tc.psum_pool(name="acc", bufs=3))
        turn_pool = ctx.enter_context(tc.psum_pool(name="turn", bufs=1))
        y_pool = ctx.enter_context(tc.psum_pool(name="y", bufs=4))

        def held(shape, dtype, name, tag=None):
            return keep.tile(shape, dtype, name=name, tag=tag or name, align_bytes=64)

        offsets = keep.tile([P, E * C // 16], U16, name="offsets")
        x_early = held([P, EARLY, T], I32, "x_early")
        xs = held([P, PASSES, T], U8, "xs")
        w1s_first = held([P, PASSES, H], U8, "w1s_first")
        w1s_rest = held([P, E * PASSES, H], U8, "w1s_rest")
        w1s = [w1s_first[:], w1s_rest[:, 0:PASSES, :], w1s_rest[:, PASSES:, :]]
        w2s = held([P, E + 1, N], U8, "w2s")
        windows = [held([P, T], F32, "window%d" % c) for c in range(NT)]
        zeros = [held([P, EDGE], F32, "zero%d" % z, "slot%d" % z) for z in range(5)]
        zero_col = held([P, 1], F32, "zero_col")
        ident = held([P, P], F32, "ident")

        def zero(engine, tile):
            engine.memset(tile[:].bitcast(I32), 0)

        def load_planes(queue, tile, rows):
            by_r = rows.rearrange("s (q r) w -> r q s w", r=4)
            for r in range(4):
                queue.dma_start(out=tile[r:P:32, :, :].bitcast(I32), in_=by_r[r].bitcast(I32))

        def load_x(dst, lo, hi):
            nc.sync.dma_start(out=dst, in_=x_words[lo:hi].rearrange("o p t r -> p o (t r)").bitcast(I32))

        def load_words(dst, words):
            nc.sync.dma_start(out=dst.bitcast(I32), in_=words.rearrange("s p b -> p s b").bitcast(I32))

        def load_gate(dst, rows, cols):
            nc.sync.dma_start(out=dst, in_=gate[rows, cols].rearrange("(c p) j -> p c j", p=P))

        nc.gpsimd.memset(zero_col[:], 0.0)
        for z in range(5):
            nc.gpsimd.memset(zeros[z][:], 0.0)

        def free_slot(engine, z):
            engine.tensor_copy(windows[z % 2][:, z // 2 * EDGE : (z // 2 + 1) * EDGE], zeros[z][:])

        make_identity(nc, ident[:])
        zero(nc.vector, xs)
        free_slot(nc.vector, 0)
        free_slot(nc.vector, 1)
        zero(nc.vector, w1s_first)
        zero(nc.vector, w2s)
        zero(nc.vector, w1s_rest)
        for z in (2, 4, 3):
            free_slot(nc.vector, z)
        for c, first in enumerate([3 * EDGE, 2 * EDGE, 0, 0]):
            nc.scalar.activation(out=windows[c][:, first:T], in_=zero_col[:].to_broadcast([P, T - first]), func=GELU)

        nc.sync.dma_start(offsets[:], offs)
        load_x(x_early[:, 0:1, :], 0, 1)
        load_x(x_early[:, 1:EARLY, :], 1, EARLY)
        load_planes(nc.sync, xs, x_scales)
        load_planes(nc.gpsimd, w2s, w2_scales.rearrange("e s q n -> (e s) q n"))
        w1_first = held([P, PASSES, 2 * H], U8, "w1_first", "slot0")
        load_words(w1_first[:], w1_words[0])
        x_late = held([P, PASSES - EARLY, T], I32, "x_late", "slot1")
        load_x(x_late[:], EARLY, PASSES)
        load_planes(nc.sync, w1s_first, w1_scales[0])
        xw = [x_early[:, o, :] for o in range(EARLY)] + [x_late[:, o, :] for o in range(PASSES - EARLY)]
        load_planes(nc.sync, w1s_rest, w1_scales[1:].rearrange("e s q i -> (e s) q i"))
        w_shared = held([P, PASSES + E + 1, 2 * H], U8, "w_shared", "slot2")
        w2w = w_shared[:, PASSES:, :]
        load_words(w_shared[:, 0:PASSES, :], w1_words[SHARED])
        load_words(w2w, w2_words[:, 0])
        gate_first = held([P, 2, C], F32, "gate_first", "slot4")
        load_gate(gate_first[:], slice(0, 2 * P), slice(0, C))
        w1_second = held([P, PASSES, 2 * H], U8, "w1_second", "slot3")
        load_words(w1_second[:], w1_words[1])
        w1w = [w1_first[:], w1_second[:], w_shared[:, 0:PASSES, :]]
        x_planes = [xs[:, o, :] for o in range(PASSES)]

        def slots_of(e):
            return offsets[:, e * C // 16 : (e + 1) * C // 16]

        def gather_words(e, o, dst):
            nc.vector.tensor_copy(dst.bitcast(U32), xw[o].bitcast(U32).indirect(slots_of(e)))

        def gather_scales(e, o, dst):
            nc.vector.tensor_copy(dst, x_planes[o].indirect(slots_of(e)))

        def first_layer(e, words, planes, col0, pass_major):
            accs = [acc_pool.tile([P, H], F32, name="acc") for j in range(2)]
            order = [(o, j) for o in range(PASSES) for j in range(2)]
            if not pass_major:
                order = [(o, j) for j in range(2) for o in range(PASSES)]
            for o, j in order:
                cols = slice(col0 + j * P, col0 + (j + 1) * P)
                nc.tensor.matmul_mx(
                    out=accs[j][:],
                    lhsT=words[o][:, cols].bitcast(FP8X4),
                    lhsT_scale=planes[o][:, cols],
                    rhs=w1w[e][:, o, :].bitcast(FP4X4),
                    rhs_scale=w1s[e][:, o, :],
                    start=(o == 0),
                    stop=(o == PASSES - 1),
                )
            return accs

        def turn(accs, grouped):
            turned = turn_pool.tile([P, 2, 2, P], F32, name="turned")
            for j in range(2):
                h = stage.tile([P, H], BF16, name="h", align_bytes=64)
                nc.scalar.activation(
                    out=h[:].rearrange("q (u p d) -> q u p d", u=2, d=2),
                    in_=accs[j][:].rearrange("q (p u d) -> q u p d", u=2, d=2),
                    func=GELU,
                )
                pairs = h[:].bitcast(F32)
                for u in range(2):
                    nc.tensor.transpose(turned[:, j, u, :], pairs[:, u * P : (u + 1) * P], ident[:])
            nc.scalar.copy(
                out=grouped[:].bitcast(F32).rearrange("p (j t u) -> p j t u", j=2, u=2),
                in_=turned[:].rearrange("p j u t -> p j t u"),
            )
            return grouped

        def quantise(grouped, codes, scales):
            nc.vector.quantize_mx(out=codes.bitcast(FP8X4), scales=scales, in_=grouped[:])

        def second_layer(e, c, dst, codes, scales):
            nc.tensor.matmul_mx(
                out=dst,
                lhsT=w2w[:, e, 2 * c * P : 2 * (c + 1) * P].bitcast(FP4X4),
                lhsT_scale=w2s[:, e, c * P : (c + 1) * P],
                rhs=codes.bitcast(FP8X4),
                rhs_scale=scales,
                start=True,
                stop=True,
            )

        y_slots = {}

        def routed_second(e, grouped, tag):
            codes = held([P, C], U32, "codes%d" % e, tag)
            scales = held([P, C], U8, "scales%d" % e)
            quantise(grouped, codes[:], scales[:])
            for b in range(2):
                bank = y_pool.tile([P, 2, C], F32, name="y")
                for i in range(2):
                    second_layer(e, 2 * b + i, bank[:, i, :], codes[:], scales[:])
                y = held([P, 2, C], F32, "y_slots%d_%d" % (e, b))
                nc.scalar.copy(out=y[:], in_=bank[:])
                for i in range(2):
                    y_slots[e, 2 * b + i] = y[:, i, :]

        def scatter(e, c):
            nc.vector.tensor_tensor(windows[c][:].indirect(slots_of(e)), y_slots[e, c], gates[e, c], MULT)

        def shared_first(g):
            return first_layer(SHARED, xw, x_planes, g * GROUP, False)

        def shared_turn(g, accs):
            return turn(accs, held([P, 4 * GROUP], BF16, "grouped_shared%d" % g))

        words_both = [held([P, E * C], I32, "words_both%d" % o) for o in range(EARLY)]
        words0 = [t[:, 0:C] for t in words_both] + [held([P, C], I32, "words0_%d" % o)[:] for o in range(EARLY, PASSES)]
        planes0 = [held([P, C], U8, "planes0_%d" % o)[:] for o in range(PASSES)]
        for o in range(EARLY):
            nc.vector.tensor_copy(words_both[o][:].bitcast(U32), xw[o].bitcast(U32).indirect(offsets[:]))
        for o in range(PASSES):
            gather_scales(0, o, planes0[o])
        for o in range(EARLY, PASSES):
            gather_words(0, o, words0[o])
        accs = first_layer(0, words0, planes0, 0, True)
        routed_second(0, turn(accs, held([P, 4 * C], BF16, "grouped_routed0")), None)
        planes1_all = held([P, PASSES, C], U8, "planes1", "planes0_2")
        words1_late = held([P, PASSES - EARLY, C], I32, "words1_late", "grouped_routed0")
        words1 = [t[:, C : E * C] for t in words_both] + [words1_late[:, o, :] for o in range(PASSES - EARLY)]
        planes1 = [planes1_all[:, o, :] for o in range(PASSES)]
        for o in range(PASSES):
            gather_scales(1, o, planes1[o])
        for o in range(EARLY, PASSES):
            gather_words(1, o, words1[o])
        gate_tiles = [gate_first]
        for name, tag, rows, cols in [
            ("gate_b", "slot0", slice(2 * P, 4 * P), slice(0, C)),
            ("gate_c", "words0_3", slice(0, 2 * P), slice(C, E * C)),
            ("gate_d", "words0_4", slice(2 * P, 4 * P), slice(C, E * C)),
        ]:
            tile = held([P, 2, C], F32, name, tag)
            load_gate(tile[:], rows, cols)
            gate_tiles.append(tile)
        gates = {}
        for e in range(E):
            for c in range(NT):
                gates[e, c] = gate_tiles[2 * e + c // 2][:, c % 2, :]

        grouped_s0 = shared_turn(0, shared_first(0))
        grouped_e1 = turn(first_layer(1, words1, planes1, 0, True), held([P, 4 * C], BF16, "grouped_routed1"))
        accs_s1 = shared_first(1)
        scatter(0, 0)
        scatter(0, 1)
        scatter(0, 2)
        routed_second(1, grouped_e1, "y_slots0_0")
        scatter(0, 3)
        grouped_s1 = shared_turn(1, accs_s1)
        accs_s2 = shared_first(2)
        grouped_s2 = shared_turn(2, accs_s2)
        scatter(1, 0)
        wide = slice(0, 2 * GROUP)
        rest = slice(2 * GROUP, T)
        codes_wide = held([P, 2 * GROUP], U32, "codes_wide", "y_slots0_1")
        scales_wide = held([P, 2 * GROUP], U8, "scales_wide")
        for g, grouped in enumerate([grouped_s0, grouped_s1]):
            cols = slice(g * GROUP, (g + 1) * GROUP)
            quantise(grouped, codes_wide[:, cols], scales_wide[:, cols])
        ys_wide = []
        for c in range(NT):
            bank = y_pool.tile([P, 2 * GROUP], F32, name="y")
            second_layer(SHARED, c, bank[:], codes_wide[:], scales_wide[:])
            ys_wide.append(bank[:])
        scatter(1, 1)
        scatter(1, 2)
        codes_rest = held([P, GROUP], U32, "codes_rest", "y_slots1_0")
        scales_rest = held([P, GROUP], U8, "scales_rest")
        quantise(grouped_s2, codes_rest[:], scales_rest[:])
        ys_rest = []
        for b in range(2):
            bank = acc_pool.tile([P, 2, GROUP], F32, name="acc")
            for i in range(2):
                second_layer(SHARED, 2 * b + i, bank[:, i, :], codes_rest[:], scales_rest[:])
                ys_rest.append(bank[:, i, :])
        res = [held([P, T], F32, "res%d" % c) for c in range(NT)]

        def finish(c, cols, ys):
            nc.vector.tensor_tensor(res[c][:, cols], ys, windows[c][:, cols], ADD)
            nc.sync.dma_start(out=out[c * P : (c + 1) * P, cols], in_=res[c][:, cols])

        for c in range(NT - 1):
            finish(c, wide, ys_wide[c])
        for c in range(NT - 1):
            finish(c, rest, ys_rest[c])
        scatter(1, NT - 1)
        finish(NT - 1, wide, ys_wide[NT - 1])
        finish(NT - 1, rest, ys_rest[NT - 1])
